import numpy as np
import ml_dtypes


def mxq(x, axis, fmt="e4m3"):
    dtype, down = {"e4m3": (ml_dtypes.float8_e4m3fn, 7), "e5m2": (ml_dtypes.float8_e5m2, 14)}[fmt]
    v = np.moveaxis(np.asarray(x, np.float32).astype(ml_dtypes.bfloat16).astype(np.float64), axis, -1)
    blocks = v.reshape(v.shape[:-1] + (-1, 32))
    amax = np.abs(blocks).max(-1, keepdims=True)
    byte = np.maximum(np.where(amax > 0, np.frexp(amax)[1] - 1 + 127, 0) - down, 1)
    scale = np.exp2(byte - 127.0)
    codes = (blocks / scale).astype(np.float32).astype(dtype).astype(np.float64)
    return np.moveaxis((codes * scale).reshape(v.shape), -1, axis)


WIDE = False


def mx_kscale(k):
    if not WIDE:
        return np.ones(k)
    levels = np.array([10, -10, 5, -5, 0])
    if k % 512:
        return np.exp2(np.random.permutation(np.resize(levels, k // 32))).repeat(32)
    a = np.empty((k // 512, 16))
    for p in range(k // 512):
        a[p, :8] = np.random.permutation(np.resize(levels, 8))
        for g in range(8):
            far = levels[np.abs(levels - a[p, g]) >= 10]
            a[p, g + 8] = far[np.random.randint(len(far))]
    return np.exp2(a.ravel()).repeat(32)


def f64(x):
    return np.asarray(x).astype(np.float64)


def striped(idx):
    return np.tile(idx.reshape(-1, 16).T, (8, 1)).astype(np.uint16)


def unstriped(offs):
    return offs[:16].T.reshape(-1).astype(np.int64)


def striped8(idx):
    return np.concatenate([x.reshape(-1, 16).T for x in idx]).astype(np.uint16)


def runs(offs, k):
    lists = np.stack([offs[16 * r : 16 * r + 16].T.reshape(-1) for r in range(8)]).astype(np.int64)
    return lists[np.arange(k) % 512 // 64]


def pack_weight(w):
    k, n = w.shape
    w = f64(np.asarray(w, np.float32).astype(ml_dtypes.bfloat16)).reshape(k // 32, 32, n)
    amax = np.abs(w).max(1)
    byte = np.clip(np.where(amax > 0, np.frexp(amax)[1] - 1 + 127 - 7, 1), 1, 254)
    scaled = (w * np.exp2(127.0 - byte)[:, None, :]).reshape(k, n).astype(np.float32)
    words = np.ascontiguousarray(scaled.reshape(k // 512, 128, 4, n).transpose(0, 1, 3, 2)).astype(ml_dtypes.float8_e4m3fn).view(np.uint8)
    return words, np.ascontiguousarray(byte.astype(np.uint8).reshape(k // 512, 16, n))


def unpack_weight(words, scales):
    g, p, n, _ = words.shape
    vals = np.ascontiguousarray(words).view(ml_dtypes.float8_e4m3fn).astype(np.float64) * np.repeat(np.exp2(scales.astype(np.float64) - 127.0), 8, axis=1)[..., None]
    return vals.transpose(0, 1, 3, 2).reshape(g * 512, n)

def planes(y):
    n, m = y.shape
    v = y.astype(np.float32).astype(ml_dtypes.bfloat16).astype(np.float64).reshape(n // 32, 32, m)
    top = np.abs(v).max(1)
    byte = np.clip(np.where(top > 0, np.frexp(top)[1] - 1 + 127 - 7, 1), 1, 254)
    codes = (v * np.exp2(127.0 - byte)[:, None, :]).reshape(n, m).astype(np.float32).astype(ml_dtypes.float8_e4m3fn).view(np.uint8)
    words = codes.reshape(n // 512, 128, 4, m).transpose(0, 1, 3, 2)
    return np.ascontiguousarray(words), np.ascontiguousarray(byte.astype(np.uint8).reshape(n // 512, 16, m))


K, T, S, N, H = 512, 2048, 256, 512, 512


def setup_inputs():
    n = np.random.standard_normal
    s = mx_kscale(K)[:, None]
    u = mx_kscale(H)
    packed_xT = pack_weight(n((K, T)) * s)
    packed_w1 = pack_weight(n((K, H)) / np.sqrt(K) / s)
    packed_w2 = pack_weight(n((K, H)) / np.sqrt(K) / s)
    packed_w3 = pack_weight(n((H, N)) / np.sqrt(H) / u[:, None])
    return {
        "x_words": packed_xT[0],
        "x_scales": packed_xT[1],
        "w1_words": packed_w1[0],
        "w1_scales": packed_w1[1],
        "w2_words": packed_w2[0],
        "w2_scales": packed_w2[1],
        "gn": (np.random.uniform(0.5, 1.5, (H, 1)) * u[:, None]).astype(np.float32),
        "w3_words": packed_w3[0],
        "w3_scales": packed_w3[1],
        "offs": striped(np.random.permutation(T)[:S]),
        "two": striped(np.random.permutation(T)[:S]),
        "n1": striped8(np.stack([np.random.permutation(S) for _ in range(8)])),
        "n2": striped8(np.stack([np.random.permutation(S) for _ in range(8)])),
        "n3": striped(np.random.permutation(S)),
    }


def reference(x_words, x_scales, w1_words, w1_scales, w2_words, w2_scales, gn, w3_words, w3_scales, offs, two, n1, n2, n3):
    xq = unpack_weight(x_words, x_scales)[:, unstriped(offs)]
    y = unpack_weight(w1_words, w1_scales).T @ xq
    x_two = unpack_weight(x_words, x_scales)[:, unstriped(two)]
    d = unpack_weight(w2_words, w2_scales).T @ x_two
    z = f64(gn) * ((y - (y[np.arange(H)[:, None], runs(n1, H)])) / (np.abs(d) + np.abs(d[np.arange(H)[:, None], runs(n2, H)]) + 0.5))
    h = unpack_weight(w3_words, w3_scales).T @ mxq(z, 0, "e4m3")
    st = h - h[:, unstriped(n3)]
    out_0 = st - (0.5 * st[:, unstriped(n3)])
    return (out_0,) + planes(out_0)

@@ -1,0 +1,220 @@
+from contextlib import ExitStack
+
+import concourse.mybir as mybir
+
+K, T, S, H, N = 512, 2048, 256, 512, 512
+FLOPS = 2 * S * (K * H + K * H + H * N)
+
+F32 = mybir.dt.float32
+BF16 = mybir.dt.bfloat16
+I32 = mybir.dt.int32
+U32 = mybir.dt.uint32
+U16 = mybir.dt.uint16
+U8 = mybir.dt.uint8
+FP8X4 = mybir.dt.float8_e4m3fn_x4
+ALU = mybir.AluOpType
+ACT = mybir.ActivationFunctionType
+
+P = 128
+PACK = 4
+HALF = S // 2
+LIST_COLS = S // 16
+
+
+def tile_picked_twlnormbtwice_none_po_kernel(
+    tc, x_words, x_scales, w1_words, w1_scales, w2_words, w2_scales, gn, w3_words, w3_scales,
+    offs, two, n1, n2, n3, out_0, out_1, out_2,
+):
+    nc = tc.nc
+
+    with ExitStack() as ctx:
+        lists = ctx.enter_context(tc.tile_pool(name="lists", bufs=1))
+        keep = ctx.enter_context(tc.tile_pool(name="keep", bufs=1))
+        psum = ctx.enter_context(tc.psum_pool(name="psum", bufs=1))
+
+        def load_list(name, src):
+            tile = lists.tile([P, LIST_COLS], U16, name=name)
+            nc.sync.dma_start(tile[:], src)
+            return tile
+
+        def words_view(words):
+            return words[0].rearrange("p n t -> p (n t)").bitcast(I32)
+
+        def load_scale_rows(engines, tile, row, scales):
+            for q in range(4):
+                engines[q].dma_start(
+                    tile[32 * q + row : 32 * q + row + 4, :].bitcast(I32),
+                    scales[0, 4 * q : 4 * q + 4, :].bitcast(I32),
+                )
+
+        def zeroed_plane(engine, name, width):
+            tile = keep.tile([P, width], U8, name=name, align_bytes=64)
+            engine.memset(tile[:].bitcast(I32), 0)
+            return tile
+
+        def deal_words(engine, name, raw):
+            dealt = keep.tile([P, H], I32, name=name, align_bytes=64)
+            engine.tensor_copy(
+                out=dealt[:].rearrange("p (t c i) -> p c t i", t=PACK, i=4),
+                in_=raw[:].rearrange("p (c i t) -> p c t i", t=PACK, i=4),
+            )
+            return dealt
+
+        def deal_scales(engine, name, raw):
+            dealt = keep.tile([P, H], U8, name=name, align_bytes=64)
+            engine.tensor_copy(
+                out=dealt[:].rearrange("p (t c i) -> p c t i", t=PACK, i=16),
+                in_=raw[:].rearrange("p (c i t) -> p c t i", t=PACK, i=16),
+            )
+            return dealt
+
+        def half_cols(h):
+            return slice(h * HALF, (h + 1) * HALF)
+
+        def half_list(tile, h):
+            return tile[:, h * LIST_COLS // 2 : (h + 1) * LIST_COLS // 2]
+
+        def fetch(out, window, offsets):
+            nc.scalar.activation(out, window[:].indirect(offsets), ACT.Copy)
+
+        def interleaved(tile):
+            return tile[:].rearrange("p (c i t) -> p c t i", t=PACK, i=4)
+
+        def by_fours(tile, h):
+            return tile[:, :, half_cols(h)].rearrange("p t (c i) -> p c t i", i=4)
+
+        xs = zeroed_plane(nc.vector, "xs", T)
+        ws_raw = zeroed_plane(nc.vector, "ws_raw", H)
+        w1s_raw = zeroed_plane(nc.vector, "w1s_raw", H)
+
+        def load_words(engine, words, name):
+            raw = keep.tile([P, H], I32, name=name, tag=name)
+            engine.dma_start(raw[:], words_view(words))
+            return raw
+
+        w2w_raw = load_words(nc.scalar, w2_words, "ww_raw")
+        w1w_raw = load_words(nc.scalar, w1_words, "w1w_raw")
+        two_t = load_list("two", two)
+        offs_t = load_list("offs", offs)
+        n2_t = load_list("n2", n2)
+        n1_t = load_list("n1", n1)
+        n3_t = load_list("n3", n3)
+        xw = keep.tile([P, T], U32, name="xw", align_bytes=64)
+        nc.sync.dma_start(xw[:].bitcast(I32), words_view(x_words))
+        load_scale_rows([nc.scalar] * 4, xs, 0, x_scales)
+        load_scale_rows([nc.scalar] * 3 + [nc.gpsimd], ws_raw, 0, w2_scales)
+        load_scale_rows([nc.gpsimd] * 4, w1s_raw, 0, w1_scales)
+
+        def pick_scales(name, offsets):
+            tile = keep.tile([P, S], U8, name=name, align_bytes=64)
+            nc.vector.tensor_copy(tile[:], xs[:].indirect(offsets[:]))
+            return tile
+
+        def pick_words(name, offsets):
+            tile = keep.tile([P, S], U32, name=name, align_bytes=64)
+            nc.vector.tensor_copy(tile[:], xw[:].indirect(offsets[:]))
+            return tile
+
+        w2w = deal_words(nc.vector, "w2w", w2w_raw)
+        w1w = deal_words(nc.vector, "w1w", w1w_raw)
+        gain = keep.tile([P, PACK], F32, name="gain", tag="w1w_raw")
+        nc.sync.dma_start(gain[:], gn.rearrange("(p t) o -> p (t o)", t=PACK))
+        w3w_raw = load_words(nc.sync, w3_words, "ww_raw")
+        xs_two = pick_scales("xs_two", two_t)
+        w2s = deal_scales(nc.vector, "w2s", ws_raw)
+        xw_two = pick_words("xw_two", two_t)
+        load_scale_rows([nc.sync] * 4, ws_raw, 0, w3_scales)
+        xs_idx = pick_scales("xs_idx", offs_t)
+        xw_idx = pick_words("xw_idx", offs_t)
+
+        def product(out, ww, ws, row, t, xwords, xscales):
+            cols = slice(t * P, (t + 1) * P)
+            nc.tensor.matmul_mx(
+                out=out, lhsT=ww[:, cols].bitcast(FP8X4), lhsT_scale=ws[row:P, cols],
+                rhs=xwords.bitcast(FP8X4), rhs_scale=xscales, start=True, stop=True,
+            )
+
+        d_ps = [psum.tile([P, S], F32, name="dh%d" % t) for t in range(PACK)]
+        y_ps = [psum.tile([P, S], F32, name="y%d" % t) for t in range(PACK)]
+        for t in range(PACK):
+            product(d_ps[t][:], w2w, w2s, 0, t, xw_two[:], xs_two[:])
+        w1s = deal_scales(nc.vector, "w2s", w1s_raw)
+        for t in range(PACK):
+            product(y_ps[t][:], w1w, w1s, 0, t, xw_idx[:], xs_idx[:])
+
+        absd = [keep.tile([P, S], F32, name="absd%d" % t) for t in range(PACK)]
+        ys = [keep.tile([P, S], F32, name="ys%d" % t) for t in range(PACK)]
+        dg = keep.tile([P, PACK, S], F32, name="dg")
+        den = keep.tile([P, PACK, S], F32, name="den")
+        root = keep.tile([P, PACK, S], F32, name="root")
+        fac = keep.tile([P, PACK, S], F32, name="fac")
+        yg = keep.tile([P, PACK, S], F32, name="yg")
+        num = keep.tile([P, PACK, S], F32, name="num")
+
+        for t in range(PACK):
+            nc.scalar.activation(absd[t][:], d_ps[t][:], ACT.Abs)
+        for t in range(PACK):
+            for h in range(2):
+                fetch(dg[:, t, half_cols(h)], absd[t], half_list(n2_t, h))
+            nc.vector.scalar_tensor_tensor(
+                out=den[:, t, :], in0=dg[:, t, :], scalar=0.5, in1=absd[t][:], op0=ALU.add, op1=ALU.add
+            )
+        for t in range(PACK):
+            nc.vector.tensor_copy(ys[t][:], y_ps[t][:])
+        for t in range(PACK):
+            nc.scalar.activation(root[:, t, :], den[:, t, :], ACT.Abs_reciprocal_sqrt)
+            nc.vector.scalar_tensor_tensor(
+                out=fac[:, t, :], in0=root[:, t, :], scalar=gain[:, t : t + 1], in1=root[:, t, :],
+                op0=ALU.mult, op1=ALU.mult,
+            )
+
+        w3w = deal_words(nc.vector, "w2w", w3w_raw)
+        w3s = deal_scales(nc.vector, "w2s", ws_raw)
+        h_ps = [psum.tile([P, S], F32, name="dh%d" % t) for t in range(PACK)]
+        for h in range(2):
+            cols = half_cols(h)
+            for t in range(PACK):
+                fetch(yg[:, t, cols], ys[t], half_list(n1_t, h))
+                nc.vector.tensor_tensor(num[:, t, cols], y_ps[t][:, cols], yg[:, t, cols], ALU.subtract)
+            zb = keep.tile([P, PACK * HALF], BF16, name="zb%d" % h, align_bytes=64)
+            nc.vector.tensor_tensor(interleaved(zb), by_fours(num, h), by_fours(fac, h), ALU.mult)
+            zw = keep.tile([P, HALF], U32, name="zw%d" % h, align_bytes=64)
+            zs = keep.tile([P, HALF], U8, name="zs%d" % h, align_bytes=64)
+            nc.vector.quantize_mx(out=zw[:].bitcast(FP8X4), scales=zs[:], in_=zb[:])
+            for t in range(PACK):
+                product(h_ps[t][:, cols], w3w, w3s, 0, t, zw[:], zs[:])
+
+        hs = [keep.tile([P, S], F32, name="hs%d" % t) for t in range(PACK)]
+        st = [keep.tile([P, S], F32, name="st%d" % t) for t in range(PACK)]
+        hg = keep.tile([P, PACK, S], F32, name="hg")
+        sg = keep.tile([P, PACK, S], F32, name="sg")
+        for t in range(PACK):
+            nc.vector.tensor_copy(hs[t][:], h_ps[t][:])
+        for t in range(PACK):
+            for h in range(2):
+                fetch(hg[:, t, half_cols(h)], hs[t], half_list(n3_t, h))
+            nc.vector.tensor_tensor(st[t][:], h_ps[t][:], hg[:, t, :], ALU.subtract)
+
+        out_rows = out_0.rearrange("(p t) j -> p t j", t=PACK)
+        ow = keep.tile([P, S], U32, name="ow", align_bytes=64)
+        osc = keep.tile([P, S], U8, name="osc", align_bytes=64)
+        res = keep.tile([P, PACK, S], F32, name="res")
+        for h in range(2):
+            cols = half_cols(h)
+            for t in range(PACK):
+                fetch(sg[:, t, cols], st[t], half_list(n3_t, h))
+                nc.vector.scalar_tensor_tensor(
+                    out=res[:, t, cols], in0=sg[:, t, cols], scalar=-0.5, in1=st[t][:, cols],
+                    op0=ALU.mult, op1=ALU.add,
+                )
+            nc.sync.dma_start(out_rows[:, :, cols], res[:, :, cols])
+            ob = keep.tile([P, PACK * HALF], BF16, name="ob%d" % h, align_bytes=64)
+            nc.vector.tensor_copy(interleaved(ob), by_fours(res, h))
+            nc.vector.quantize_mx(out=ow[:, cols].bitcast(FP8X4), scales=osc[:, cols], in_=ob[:])
+            nc.sync.dma_start(words_view(out_1)[:, cols], ow[:, cols].bitcast(I32))
+        for q in range(4):
+            engine = nc.scalar if q % 2 == 0 else nc.sync
+            engine.dma_start(
+                out_2[0, 4 * q : 4 * q + 4, :].bitcast(I32),
+                osc[32 * q : 32 * q + 4, :].bitcast(I32),
+            )

@@ -17,7 +17,9 @@ ACT = mybir.ActivationFunctionType
 
 P = 128
 PACK = 4
+SPARE = 8
 HALF = S // 2
+HALVES = (slice(0, HALF), slice(HALF, S))
 LIST_COLS = S // 16
 
 
@@ -48,7 +50,7 @@ def tile_picked_twlnormbtwice_none_po_kernel(
                 )
 
         def zeroed_plane(engine, name, width):
-            tile = keep.tile([P, width], U8, name=name, align_bytes=64)
+            tile = keep.tile([P, width], U8, name=name, tag=name, align_bytes=64)
             engine.memset(tile[:].bitcast(I32), 0)
             return tile
 
@@ -68,24 +70,23 @@ def tile_picked_twlnormbtwice_none_po_kernel(
             )
             return dealt
 
-        def half_cols(h):
-            return slice(h * HALF, (h + 1) * HALF)
-
-        def half_list(tile, h):
-            return tile[:, h * LIST_COLS // 2 : (h + 1) * LIST_COLS // 2]
+        def list_cols(tile, cols):
+            return tile[:, cols.start // 16 : cols.stop // 16]
 
         def fetch(out, window, offsets):
-            nc.scalar.activation(out, window[:].indirect(offsets), ACT.Copy)
+            nc.scalar.activation(out, window.indirect(offsets), ACT.Copy)
 
         def interleaved(tile):
             return tile[:].rearrange("p (c i t) -> p c t i", t=PACK, i=4)
 
-        def by_fours(tile, h):
-            return tile[:, :, half_cols(h)].rearrange("p t (c i) -> p c t i", i=4)
+        def by_fours(tile, cols):
+            return tile[:, :, cols].rearrange("p t (c i) -> p c t i", i=4)
 
         xs = zeroed_plane(nc.vector, "xs", T)
-        ws_raw = zeroed_plane(nc.vector, "ws_raw", H)
-        w1s_raw = zeroed_plane(nc.vector, "w1s_raw", H)
+        w2s_raw = zeroed_plane(nc.vector, "w2s_raw", H)
+        one = keep.tile([P, 1], F32, name="one")
+        nc.vector.memset(one[:], 1.0)
+        w13s_raw = zeroed_plane(nc.vector, "w13s_raw", H)
 
         def load_words(engine, words, name):
             raw = keep.tile([P, H], I32, name=name, tag=name)
@@ -101,31 +102,29 @@ def tile_picked_twlnormbtwice_none_po_kernel(
         n3_t = load_list("n3", n3)
         xw = keep.tile([P, T], U32, name="xw", align_bytes=64)
         nc.sync.dma_start(xw[:].bitcast(I32), words_view(x_words))
-        load_scale_rows([nc.scalar] * 4, xs, 0, x_scales)
-        load_scale_rows([nc.scalar] * 3 + [nc.gpsimd], ws_raw, 0, w2_scales)
-        load_scale_rows([nc.gpsimd] * 4, w1s_raw, 0, w1_scales)
+        load_scale_rows([nc.scalar, nc.sync] * 2, xs, 0, x_scales)
+        load_scale_rows([nc.scalar, nc.sync, nc.scalar, nc.gpsimd], w2s_raw, 0, w2_scales)
+        warm = keep.tile([P, 1], F32, name="warm")
+        nc.scalar.activation(warm[:], one[:], ACT.Abs_reciprocal_sqrt)
+        load_scale_rows([nc.sync, nc.scalar] * 2, w13s_raw, 0, w1_scales)
+        load_scale_rows([nc.sync, nc.scalar] * 2, w13s_raw, 4, w3_scales)
 
-        def pick_scales(name, offsets):
-            tile = keep.tile([P, S], U8, name=name, align_bytes=64)
+        absd = [keep.tile([P, 2 * S], F32, name="absd%d" % t) for t in range(PACK)]
+        hs = [keep.tile([P, S + SPARE], F32, name="hs%d" % t) for t in range(PACK)]
+        for t in range(PACK):
+            nc.vector.memset(absd[t][:, S:], 0.0)
+        for t in range(PACK):
+            nc.vector.memset(hs[t][:, S:], 0.0)
+
+        def pick_scales(offsets):
+            tile = keep.tile([P, S], U8, name="xs_picked", align_bytes=64)
             nc.vector.tensor_copy(tile[:], xs[:].indirect(offsets[:]))
             return tile
 
-        def pick_words(name, offsets):
-            tile = keep.tile([P, S], U32, name=name, align_bytes=64)
+        def pick_words(offsets, tag):
+            tile = keep.tile([P, S], U32, name="xw_picked", tag=tag, align_bytes=64)
             nc.vector.tensor_copy(tile[:], xw[:].indirect(offsets[:]))
             return tile
-
-        w2w = deal_words(nc.vector, "w2w", w2w_raw)
-        w1w = deal_words(nc.vector, "w1w", w1w_raw)
-        gain = keep.tile([P, PACK], F32, name="gain", tag="w1w_raw")
-        nc.sync.dma_start(gain[:], gn.rearrange("(p t) o -> p (t o)", t=PACK))
-        w3w_raw = load_words(nc.sync, w3_words, "ww_raw")
-        xs_two = pick_scales("xs_two", two_t)
-        w2s = deal_scales(nc.vector, "w2s", ws_raw)
-        xw_two = pick_words("xw_two", two_t)
-        load_scale_rows([nc.sync] * 4, ws_raw, 0, w3_scales)
-        xs_idx = pick_scales("xs_idx", offs_t)
-        xw_idx = pick_words("xw_idx", offs_t)
 
         def product(out, ww, ws, row, t, xwords, xscales):
             cols = slice(t * P, (t + 1) * P)
@@ -134,15 +133,26 @@ def tile_picked_twlnormbtwice_none_po_kernel(
                 rhs=xwords.bitcast(FP8X4), rhs_scale=xscales, start=True, stop=True,
             )
 
+        w2w = deal_words(nc.vector, "w2w", w2w_raw)
+        w3w_raw = load_words(nc.sync, w3_words, "ww_raw")
+        w1w = deal_words(nc.vector, "w1w", w1w_raw)
+        gain = keep.tile([P, PACK], F32, name="gain", tag="w1w_raw")
+        nc.sync.dma_start(gain[:], gn.rearrange("(p t) o -> p (t o)", t=PACK))
+        xw_two = pick_words(two_t, "xw_two")
+        xs_two = pick_scales(two_t)
+        w2s = deal_scales(nc.vector, "ws", w2s_raw)
+
         d_ps = [psum.tile([P, S], F32, name="dh%d" % t) for t in range(PACK)]
         y_ps = [psum.tile([P, S], F32, name="y%d" % t) for t in range(PACK)]
         for t in range(PACK):
             product(d_ps[t][:], w2w, w2s, 0, t, xw_two[:], xs_two[:])
-        w1s = deal_scales(nc.vector, "w2s", w1s_raw)
-        for t in range(PACK):
-            product(y_ps[t][:], w1w, w1s, 0, t, xw_idx[:], xs_idx[:])
 
-        absd = [keep.tile([P, S], F32, name="absd%d" % t) for t in range(PACK)]
+        xw_idx = pick_words(offs_t, "w2s_raw")
+        xs_idx = pick_scales(offs_t)
+        w13s = deal_scales(nc.vector, "ws", w13s_raw)
+        for t in range(PACK):
+            product(y_ps[t][:], w1w, w13s, 0, t, xw_idx[:], xs_idx[:])
+
         ys = [keep.tile([P, S], F32, name="ys%d" % t) for t in range(PACK)]
         dg = keep.tile([P, PACK, S], F32, name="dg")
         den = keep.tile([P, PACK, S], F32, name="den")
@@ -152,68 +162,63 @@ def tile_picked_twlnormbtwice_none_po_kernel(
         num = keep.tile([P, PACK, S], F32, name="num")
 
         for t in range(PACK):
-            nc.scalar.activation(absd[t][:], d_ps[t][:], ACT.Abs)
+            nc.scalar.activation(absd[t][:, :S], d_ps[t][:], ACT.Abs)
         for t in range(PACK):
-            for h in range(2):
-                fetch(dg[:, t, half_cols(h)], absd[t], half_list(n2_t, h))
+            fetch(dg[:, t, :], absd[t][:], n2_t[:])
             nc.vector.scalar_tensor_tensor(
-                out=den[:, t, :], in0=dg[:, t, :], scalar=0.5, in1=absd[t][:], op0=ALU.add, op1=ALU.add
+                out=den[:, t, :], in0=dg[:, t, :], scalar=0.5, in1=absd[t][:, :S], op0=ALU.add, op1=ALU.add
             )
         for t in range(PACK):
-            nc.vector.tensor_copy(ys[t][:], y_ps[t][:])
-        for t in range(PACK):
-            nc.scalar.activation(root[:, t, :], den[:, t, :], ACT.Abs_reciprocal_sqrt)
-            nc.vector.scalar_tensor_tensor(
-                out=fac[:, t, :], in0=root[:, t, :], scalar=gain[:, t : t + 1], in1=root[:, t, :],
-                op0=ALU.mult, op1=ALU.mult,
-            )
+            nc.vector.tensor_scalar(ys[t][:], y_ps[t][:], gain[:, t : t + 1], None, ALU.mult)
 
         w3w = deal_words(nc.vector, "w2w", w3w_raw)
-        w3s = deal_scales(nc.vector, "w2s", ws_raw)
         h_ps = [psum.tile([P, S], F32, name="dh%d" % t) for t in range(PACK)]
-        for h in range(2):
-            cols = half_cols(h)
+        for cols in HALVES:
+            nc.scalar.activation(root[:, :, cols], den[:, :, cols], ACT.Abs_reciprocal_sqrt)
+            nc.vector.tensor_tensor(fac[:, :, cols], root[:, :, cols], root[:, :, cols], ALU.mult)
             for t in range(PACK):
-                fetch(yg[:, t, cols], ys[t], half_list(n1_t, h))
-                nc.vector.tensor_tensor(num[:, t, cols], y_ps[t][:, cols], yg[:, t, cols], ALU.subtract)
-            zb = keep.tile([P, PACK * HALF], BF16, name="zb%d" % h, align_bytes=64)
-            nc.vector.tensor_tensor(interleaved(zb), by_fours(num, h), by_fours(fac, h), ALU.mult)
-            zw = keep.tile([P, HALF], U32, name="zw%d" % h, align_bytes=64)
-            zs = keep.tile([P, HALF], U8, name="zs%d" % h, align_bytes=64)
+                fetch(yg[:, t, cols], ys[t][:], list_cols(n1_t, cols))
+                nc.vector.scalar_tensor_tensor(
+                    out=num[:, t, cols], in0=y_ps[t][:, cols], scalar=gain[:, t : t + 1], in1=yg[:, t, cols],
+                    op0=ALU.mult, op1=ALU.subtract,
+                )
+            zb = keep.tile([P, PACK * HALF], BF16, name="zb%d" % cols.start, align_bytes=64)
+            nc.vector.tensor_tensor(interleaved(zb), by_fours(num, cols), by_fours(fac, cols), ALU.mult)
+            zw = keep.tile([P, HALF], U32, name="zw%d" % cols.start, align_bytes=64)
+            zs = keep.tile([P, HALF], U8, name="zs%d" % cols.start, align_bytes=64)
             nc.vector.quantize_mx(out=zw[:].bitcast(FP8X4), scales=zs[:], in_=zb[:])
             for t in range(PACK):
-                product(h_ps[t][:, cols], w3w, w3s, 0, t, zw[:], zs[:])
+                product(h_ps[t][:, cols], w3w, w13s, 4, t, zw[:], zs[:])
+        for t in range(PACK):
+            nc.scalar.copy(hs[t][:, HALVES[0]], h_ps[t][:, HALVES[0]])
+        for t in range(PACK):
+            nc.vector.tensor_copy(hs[t][:, HALVES[1]], h_ps[t][:, HALVES[1]])
 
-        hs = [keep.tile([P, S], F32, name="hs%d" % t) for t in range(PACK)]
         st = [keep.tile([P, S], F32, name="st%d" % t) for t in range(PACK)]
         hg = keep.tile([P, PACK, S], F32, name="hg")
         sg = keep.tile([P, PACK, S], F32, name="sg")
         for t in range(PACK):
-            nc.vector.tensor_copy(hs[t][:], h_ps[t][:])
-        for t in range(PACK):
-            for h in range(2):
-                fetch(hg[:, t, half_cols(h)], hs[t], half_list(n3_t, h))
+            fetch(hg[:, t, :], hs[t][:], n3_t[:])
             nc.vector.tensor_tensor(st[t][:], h_ps[t][:], hg[:, t, :], ALU.subtract)
 
         out_rows = out_0.rearrange("(p t) j -> p t j", t=PACK)
         ow = keep.tile([P, S], U32, name="ow", align_bytes=64)
         osc = keep.tile([P, S], U8, name="osc", align_bytes=64)
         res = keep.tile([P, PACK, S], F32, name="res")
-        for h in range(2):
-            cols = half_cols(h)
+        for cols in HALVES:
             for t in range(PACK):
-                fetch(sg[:, t, cols], st[t], half_list(n3_t, h))
+                fetch(sg[:, t, cols], st[t][:], list_cols(n3_t, cols))
                 nc.vector.scalar_tensor_tensor(
                     out=res[:, t, cols], in0=sg[:, t, cols], scalar=-0.5, in1=st[t][:, cols],
                     op0=ALU.mult, op1=ALU.add,
                 )
             nc.sync.dma_start(out_rows[:, :, cols], res[:, :, cols])
-            ob = keep.tile([P, PACK * HALF], BF16, name="ob%d" % h, align_bytes=64)
-            nc.vector.tensor_copy(interleaved(ob), by_fours(res, h))
+            ob = keep.tile([P, PACK * HALF], BF16, name="ob%d" % cols.start, align_bytes=64)
+            nc.vector.tensor_copy(interleaved(ob), by_fours(res, cols))
             nc.vector.quantize_mx(out=ow[:, cols].bitcast(FP8X4), scales=osc[:, cols], in_=ob[:])
             nc.sync.dma_start(words_view(out_1)[:, cols], ow[:, cols].bitcast(I32))
         for q in range(4):
-            engine = nc.scalar if q % 2 == 0 else nc.sync
+            engine = nc.sync if q == 3 else nc.scalar
             engine.dma_start(
                 out_2[0, 4 * q : 4 * q + 4, :].bitcast(I32),
                 osc[32 * q : 32 * q + 4, :].bitcast(I32),

from contextlib import ExitStack

import concourse.mybir as mybir

K, T, S, H, N = 512, 2048, 256, 512, 512
FLOPS = 2 * S * (K * H + K * H + H * N)

F32 = mybir.dt.float32
BF16 = mybir.dt.bfloat16
I32 = mybir.dt.int32
U32 = mybir.dt.uint32
U16 = mybir.dt.uint16
U8 = mybir.dt.uint8
FP8X4 = mybir.dt.float8_e4m3fn_x4
ALU = mybir.AluOpType
ACT = mybir.ActivationFunctionType

P = 128
PACK = 4
SPARE = 8
HALF = S // 2
HALVES = (slice(0, HALF), slice(HALF, S))
LIST_COLS = S // 16


def tile_picked_twlnormbtwice_none_po_kernel(
    tc, x_words, x_scales, w1_words, w1_scales, w2_words, w2_scales, gn, w3_words, w3_scales,
    offs, two, n1, n2, n3, out_0, out_1, out_2,
):
    nc = tc.nc

    with ExitStack() as ctx:
        lists = ctx.enter_context(tc.tile_pool(name="lists", bufs=1))
        keep = ctx.enter_context(tc.tile_pool(name="keep", bufs=1))
        psum = ctx.enter_context(tc.psum_pool(name="psum", bufs=1))

        def load_list(name, src):
            tile = lists.tile([P, LIST_COLS], U16, name=name)
            nc.sync.dma_start(tile[:], src)
            return tile

        def words_view(words):
            return words[0].rearrange("p n t -> p (n t)").bitcast(I32)

        def load_scale_rows(engines, tile, row, scales):
            for q in range(4):
                engines[q].dma_start(
                    tile[32 * q + row : 32 * q + row + 4, :].bitcast(I32),
                    scales[0, 4 * q : 4 * q + 4, :].bitcast(I32),
                )

        def zeroed_plane(engine, name, width):
            tile = keep.tile([P, width], U8, name=name, tag=name, align_bytes=64)
            engine.memset(tile[:].bitcast(I32), 0)
            return tile

        def deal_words(engine, name, raw):
            dealt = keep.tile([P, H], I32, name=name, align_bytes=64)
            engine.tensor_copy(
                out=dealt[:].rearrange("p (t c i) -> p c t i", t=PACK, i=4),
                in_=raw[:].rearrange("p (c i t) -> p c t i", t=PACK, i=4),
            )
            return dealt

        def deal_scales(engine, name, raw):
            dealt = keep.tile([P, H], U8, name=name, align_bytes=64)
            engine.tensor_copy(
                out=dealt[:].rearrange("p (t c i) -> p c t i", t=PACK, i=16),
                in_=raw[:].rearrange("p (c i t) -> p c t i", t=PACK, i=16),
            )
            return dealt

        def list_cols(tile, cols):
            return tile[:, cols.start // 16 : cols.stop // 16]

        def fetch(out, window, offsets):
            nc.scalar.activation(out, window.indirect(offsets), ACT.Copy)

        def interleaved(tile):
            return tile[:].rearrange("p (c i t) -> p c t i", t=PACK, i=4)

        def by_fours(tile, cols):
            return tile[:, :, cols].rearrange("p t (c i) -> p c t i", i=4)

        xs = zeroed_plane(nc.vector, "xs", T)
        w2s_raw = zeroed_plane(nc.vector, "w2s_raw", H)
        one = keep.tile([P, 1], F32, name="one")
        nc.vector.memset(one[:], 1.0)
        w13s_raw = zeroed_plane(nc.vector, "w13s_raw", H)

        def load_words(engine, words, name):
            raw = keep.tile([P, H], I32, name=name, tag=name)
            engine.dma_start(raw[:], words_view(words))
            return raw

        w2w_raw = load_words(nc.scalar, w2_words, "ww_raw")
        w1w_raw = load_words(nc.scalar, w1_words, "w1w_raw")
        two_t = load_list("two", two)
        offs_t = load_list("offs", offs)
        n2_t = load_list("n2", n2)
        n1_t = load_list("n1", n1)
        n3_t = load_list("n3", n3)
        xw = keep.tile([P, T], U32, name="xw", align_bytes=64)
        nc.sync.dma_start(xw[:].bitcast(I32), words_view(x_words))
        load_scale_rows([nc.scalar, nc.sync] * 2, xs, 0, x_scales)
        load_scale_rows([nc.scalar, nc.sync, nc.scalar, nc.gpsimd], w2s_raw, 0, w2_scales)
        warm = keep.tile([P, 1], F32, name="warm")
        nc.scalar.activation(warm[:], one[:], ACT.Abs_reciprocal_sqrt)
        load_scale_rows([nc.sync, nc.scalar] * 2, w13s_raw, 0, w1_scales)
        load_scale_rows([nc.sync, nc.scalar] * 2, w13s_raw, 4, w3_scales)

        absd = [keep.tile([P, 2 * S], F32, name="absd%d" % t) for t in range(PACK)]
        hs = [keep.tile([P, S + SPARE], F32, name="hs%d" % t) for t in range(PACK)]
        for t in range(PACK):
            nc.vector.memset(absd[t][:, S:], 0.0)
        for t in range(PACK):
            nc.vector.memset(hs[t][:, S:], 0.0)

        def pick_scales(offsets):
            tile = keep.tile([P, S], U8, name="xs_picked", align_bytes=64)
            nc.vector.tensor_copy(tile[:], xs[:].indirect(offsets[:]))
            return tile

        def pick_words(offsets, tag):
            tile = keep.tile([P, S], U32, name="xw_picked", tag=tag, align_bytes=64)
            nc.vector.tensor_copy(tile[:], xw[:].indirect(offsets[:]))
            return tile

        def product(out, ww, ws, row, t, xwords, xscales):
            cols = slice(t * P, (t + 1) * P)
            nc.tensor.matmul_mx(
                out=out, lhsT=ww[:, cols].bitcast(FP8X4), lhsT_scale=ws[row:P, cols],
                rhs=xwords.bitcast(FP8X4), rhs_scale=xscales, start=True, stop=True,
            )

        w2w = deal_words(nc.vector, "w2w", w2w_raw)
        w3w_raw = load_words(nc.sync, w3_words, "ww_raw")
        w1w = deal_words(nc.vector, "w1w", w1w_raw)
        gain = keep.tile([P, PACK], F32, name="gain", tag="w1w_raw")
        nc.sync.dma_start(gain[:], gn.rearrange("(p t) o -> p (t o)", t=PACK))
        xw_two = pick_words(two_t, "xw_two")
        xs_two = pick_scales(two_t)
        w2s = deal_scales(nc.vector, "ws", w2s_raw)

        d_ps = [psum.tile([P, S], F32, name="dh%d" % t) for t in range(PACK)]
        y_ps = [psum.tile([P, S], F32, name="y%d" % t) for t in range(PACK)]
        for t in range(PACK):
            product(d_ps[t][:], w2w, w2s, 0, t, xw_two[:], xs_two[:])

        xw_idx = pick_words(offs_t, "w2s_raw")
        xs_idx = pick_scales(offs_t)
        w13s = deal_scales(nc.vector, "ws", w13s_raw)
        for t in range(PACK):
            product(y_ps[t][:], w1w, w13s, 0, t, xw_idx[:], xs_idx[:])

        ys = [keep.tile([P, S], F32, name="ys%d" % t) for t in range(PACK)]
        dg = keep.tile([P, PACK, S], F32, name="dg")
        den = keep.tile([P, PACK, S], F32, name="den")
        root = keep.tile([P, PACK, S], F32, name="root")
        fac = keep.tile([P, PACK, S], F32, name="fac")
        yg = keep.tile([P, PACK, S], F32, name="yg")
        num = keep.tile([P, PACK, S], F32, name="num")

        for t in range(PACK):
            nc.scalar.activation(absd[t][:, :S], d_ps[t][:], ACT.Abs)
        for t in range(PACK):
            fetch(dg[:, t, :], absd[t][:], n2_t[:])
            nc.vector.scalar_tensor_tensor(
                out=den[:, t, :], in0=dg[:, t, :], scalar=0.5, in1=absd[t][:, :S], op0=ALU.add, op1=ALU.add
            )
        for t in range(PACK):
            nc.vector.tensor_scalar(ys[t][:], y_ps[t][:], gain[:, t : t + 1], None, ALU.mult)

        w3w = deal_words(nc.vector, "w2w", w3w_raw)
        h_ps = [psum.tile([P, S], F32, name="dh%d" % t) for t in range(PACK)]
        for cols in HALVES:
            nc.scalar.activation(root[:, :, cols], den[:, :, cols], ACT.Abs_reciprocal_sqrt)
            nc.vector.tensor_tensor(fac[:, :, cols], root[:, :, cols], root[:, :, cols], ALU.mult)
            for t in range(PACK):
                fetch(yg[:, t, cols], ys[t][:], list_cols(n1_t, cols))
                nc.vector.scalar_tensor_tensor(
                    out=num[:, t, cols], in0=y_ps[t][:, cols], scalar=gain[:, t : t + 1], in1=yg[:, t, cols],
                    op0=ALU.mult, op1=ALU.subtract,
                )
            zb = keep.tile([P, PACK * HALF], BF16, name="zb%d" % cols.start, align_bytes=64)
            nc.vector.tensor_tensor(interleaved(zb), by_fours(num, cols), by_fours(fac, cols), ALU.mult)
            zw = keep.tile([P, HALF], U32, name="zw%d" % cols.start, align_bytes=64)
            zs = keep.tile([P, HALF], U8, name="zs%d" % cols.start, align_bytes=64)
            nc.vector.quantize_mx(out=zw[:].bitcast(FP8X4), scales=zs[:], in_=zb[:])
            for t in range(PACK):
                product(h_ps[t][:, cols], w3w, w13s, 4, t, zw[:], zs[:])
        for t in range(PACK):
            nc.scalar.copy(hs[t][:, HALVES[0]], h_ps[t][:, HALVES[0]])
        for t in range(PACK):
            nc.vector.tensor_copy(hs[t][:, HALVES[1]], h_ps[t][:, HALVES[1]])

        st = [keep.tile([P, S], F32, name="st%d" % t) for t in range(PACK)]
        hg = keep.tile([P, PACK, S], F32, name="hg")
        sg = keep.tile([P, PACK, S], F32, name="sg")
        for t in range(PACK):
            fetch(hg[:, t, :], hs[t][:], n3_t[:])
            nc.vector.tensor_tensor(st[t][:], h_ps[t][:], hg[:, t, :], ALU.subtract)

        out_rows = out_0.rearrange("(p t) j -> p t j", t=PACK)
        ow = keep.tile([P, S], U32, name="ow", align_bytes=64)
        osc = keep.tile([P, S], U8, name="osc", align_bytes=64)
        res = keep.tile([P, PACK, S], F32, name="res")
        for cols in HALVES:
            for t in range(PACK):
                fetch(sg[:, t, cols], st[t][:], list_cols(n3_t, cols))
                nc.vector.scalar_tensor_tensor(
                    out=res[:, t, cols], in0=sg[:, t, cols], scalar=-0.5, in1=st[t][:, cols],
                    op0=ALU.mult, op1=ALU.add,
                )
            nc.sync.dma_start(out_rows[:, :, cols], res[:, :, cols])
            ob = keep.tile([P, PACK * HALF], BF16, name="ob%d" % cols.start, align_bytes=64)
            nc.vector.tensor_copy(interleaved(ob), by_fours(res, cols))
            nc.vector.quantize_mx(out=ow[:, cols].bitcast(FP8X4), scales=osc[:, cols], in_=ob[:])
            nc.sync.dma_start(words_view(out_1)[:, cols], ow[:, cols].bitcast(I32))
        for q in range(4):
            engine = nc.sync if q == 3 else nc.scalar
            engine.dma_start(
                out_2[0, 4 * q : 4 * q + 4, :].bitcast(I32),
                osc[32 * q : 32 * q + 4, :].bitcast(I32),
            )
